import numpy as np
import ml_dtypes


def mxq(x, axis, fmt="e4m3"):
    dtype, down = {"e4m3": (ml_dtypes.float8_e4m3fn, 7), "e5m2": (ml_dtypes.float8_e5m2, 14)}[fmt]
    v = np.moveaxis(np.asarray(x, np.float32).astype(ml_dtypes.bfloat16).astype(np.float64), axis, -1)
    blocks = v.reshape(v.shape[:-1] + (-1, 32))
    amax = np.abs(blocks).max(-1, keepdims=True)
    byte = np.maximum(np.where(amax > 0, np.frexp(amax)[1] - 1 + 127, 0) - down, 1)
    scale = np.exp2(byte - 127.0)
    codes = (blocks / scale).astype(np.float32).astype(dtype).astype(np.float64)
    return np.moveaxis((codes * scale).reshape(v.shape), -1, axis)


WIDE = False


def mx_kscale(k):
    if not WIDE:
        return np.ones(k)
    levels = np.array([10, -10, 5, -5, 0])
    if k % 512:
        return np.exp2(np.random.permutation(np.resize(levels, k // 32))).repeat(32)
    a = np.empty((k // 512, 16))
    for p in range(k // 512):
        a[p, :8] = np.random.permutation(np.resize(levels, 8))
        for g in range(8):
            far = levels[np.abs(levels - a[p, g]) >= 10]
            a[p, g + 8] = far[np.random.randint(len(far))]
    return np.exp2(a.ravel()).repeat(32)


def f64(x):
    return np.asarray(x).astype(np.float64)


def striped(idx):
    return np.tile(idx.reshape(-1, 16).T, (8, 1)).astype(np.uint16)


def unstriped(offs):
    return offs[:16].T.reshape(-1).astype(np.int64)


E2M1 = np.array([0.0, 0.5, 1.0, 1.5, 2.0, 3.0, 4.0, 6.0, -0.0, -0.5, -1.0, -1.5, -2.0, -3.0, -4.0, -6.0])


def pack_weight(w, fmt):
    k, n = w.shape
    w = f64(np.asarray(w, np.float32).astype(ml_dtypes.bfloat16)).reshape(k // 32, 32, n)
    amax = np.abs(w).max(1)
    if fmt == "e4m3":
        byte = np.frexp(amax)[1] - 1 + 127 - 7
    else:
        mant, ex = np.frexp(amax / 6.0)
        byte = np.where(mant > 0.5, ex, ex - 1) + 127
    byte = np.clip(np.where(amax > 0, byte, 1), 1, 254)
    scaled = (w * np.exp2(127.0 - byte)[:, None, :]).reshape(k, n).astype(np.float32)
    by_word = np.ascontiguousarray(scaled.reshape(k // 512, 128, 4, n).transpose(0, 1, 3, 2))
    if fmt == "e4m3":
        words = by_word.astype(ml_dtypes.float8_e4m3fn).view(np.uint8)
    else:
        c = by_word.astype(ml_dtypes.float4_e2m1fn).view(np.uint8) & 0xF
        words = (c[..., 0::2] | (c[..., 1::2] << 4)).reshape(k // 512, 128, 2 * n)
    return np.ascontiguousarray(words), np.ascontiguousarray(byte.astype(np.uint8).reshape(k // 512, 16, n))


def unpack_weight(words, scales, fmt):
    g, _, n = scales.shape
    words = np.ascontiguousarray(words).reshape(g, 128, n, -1)
    if fmt == "e4m3":
        vals = words.view(ml_dtypes.float8_e4m3fn).astype(np.float64)
    else:
        nib = np.empty((g, 128, n, 4), np.uint8)
        nib[..., 0::2] = words & 0xF
        nib[..., 1::2] = words >> 4
        vals = E2M1[nib]
    vals = vals * np.repeat(np.exp2(scales.astype(np.float64) - 127.0), 8, axis=1)[..., None]
    return vals.transpose(0, 1, 3, 2).reshape(g * 512, n)


def gelu(v):
    return 0.5 * v * (1.0 + np.tanh(np.sqrt(2.0 / np.pi) * (v + 0.044715 * v**3)))


def striped8(idx):
    return np.concatenate([v.reshape(-1, 16).T for v in idx]).astype(np.uint16)


def unstriped8(offs):
    return np.stack([offs[16 * g:16 * g + 16].T.reshape(-1) for g in range(8)]).astype(np.int64)


def runs(v, idx8):
    k = np.arange(v.shape[0])
    return v[k[:, None], idx8[k % 512 // 64]]


K, T, S, P, H, N = 1024, 2048, 1024, 512, 1024, 512


def setup_inputs():
    n = np.random.standard_normal
    s = mx_kscale(K)[:, None]
    u = mx_kscale(H)[:, None]
    d = {}
    d["tab_words"], d["tab_scales"] = pack_weight(n((K, T)) * s, "e4m3")
    d["offs"] = striped8(np.stack([np.random.permutation(T)[:S] for _ in range(8)]))
    d["pos1"] = striped(np.random.permutation(S)[:P])
    d["pos2"] = striped(np.random.permutation(S)[:P])
    d["w1"] = (1.3 * n((K, H)) / K**0.5 / s).astype(np.float32)
    d["b1"] = (0.6 * n(H)).astype(np.float32)
    d["gain"] = (np.exp(0.3 * n(H)) * u[:, 0]).astype(np.float32)
    d["w4_words"], d["w4_scales"] = pack_weight(1.2 * n((H, N)) / H**0.5 / u, "e2m1")
    return d


def reference(tab_words, tab_scales, offs, pos1, pos2, w1, b1, gain, w4_words, w4_scales):
    v = runs(unpack_weight(tab_words, tab_scales, "e4m3"), unstriped8(offs))
    a = mxq(f64(w1), 0, "e4m3").T @ v
    h = np.tanh(a + f64(b1)[:, None]) * f64(gain)[:, None]
    z = np.maximum(h[:, unstriped(pos1)], h[:, unstriped(pos2)])
    w4 = unpack_weight(w4_words, w4_scales, "e2m1")
    out = w4.T @ mxq(z, 0, "e4m3")
    return out

@@ -1,0 +1,205 @@
+from contextlib import ExitStack
+
+import concourse.mybir as mybir
+
+K, T, S, PAIRS, H, N = 1024, 2048, 1024, 512, 1024, 512
+FLOPS = 2 * K * H * S + 2 * H * N * PAIRS
+
+F32 = mybir.dt.float32
+BF16 = mybir.dt.bfloat16
+I32 = mybir.dt.int32
+U32 = mybir.dt.uint32
+U16 = mybir.dt.uint16
+U8 = mybir.dt.uint8
+FP8X4 = mybir.dt.float8_e4m3fn_x4
+FP4X4 = mybir.dt.float4_e2m1fn_x4
+ACT = mybir.ActivationFunctionType
+ALU = mybir.AluOpType
+
+P = 128
+PACK = 4
+K_PASS = P * PACK
+BANK = 512
+CHUNK = 128
+PLANE_ROW = 8
+
+
+def tile_list_braille_proof_scores_kernel(
+    tc, tab_words, tab_scales, offs, pos1, pos2, w1, b1, gain, w4_words, w4_scales, out
+):
+    nc = tc.nc
+    with ExitStack() as ctx:
+        lists = ctx.enter_context(tc.tile_pool(name="lists", bufs=1))
+        keep = ctx.enter_context(tc.tile_pool(name="keep", bufs=1))
+        ring = ctx.enter_context(tc.tile_pool(name="ring", bufs=2))
+        psum = ctx.enter_context(tc.psum_pool(name="psum", bufs=8))
+
+        offs_sb = lists.tile([P, S // 16], U16, name="offs_sb")
+        pos_sb = [lists.tile([P, PAIRS // 16], U16, name=f"pos{i}_sb") for i in (1, 2)]
+
+        tab_bytes = keep.tile([P, T], U8, name="tab_bytes", align_bytes=64)
+        nc.gpsimd.memset(tab_bytes[:].bitcast(I32), 0)
+        warm = keep.tile([P, 2], F32, name="warm")
+        nc.vector.memset(warm[:, 0:1], 0.0)
+        w4_planes = keep.tile([P, 2, N], U8, name="w4_planes", align_bytes=64)
+        nc.vector.memset(w4_planes[:].bitcast(I32), 0)
+
+        nc.sync.dma_start(offs_sb[:], offs)
+        nc.sync.dma_start(pos_sb[0][:], pos1)
+        nc.sync.dma_start(pos_sb[1][:], pos2)
+        scale_rows = tab_scales.rearrange("a (g e) t -> e g a t", e=2).bitcast(I32)
+        for e in range(2):
+            nc.sync.dma_start(tab_bytes[e:P:PLANE_ROW, :].bitcast(I32), scale_rows[e])
+        nc.scalar.activation(warm[:, 1:2], warm[:, 0:1], ACT.Tanh)
+
+        bias_sb = keep.tile([P, 2, PACK], F32, name="bias_sb")
+        gain_sb = keep.tile([P, 2, PACK], F32, name="gain_sb")
+        nc.gpsimd.dma_start(bias_sb[:], b1.rearrange("(b p t) -> p b t", b=2, t=PACK))
+        nc.gpsimd.dma_start(gain_sb[:], gain.rearrange("(b p t) -> p b t", b=2, t=PACK))
+        w4_rows = w4_scales.rearrange("a q n -> q a n").bitcast(I32)
+        for quad in range(4):
+            nc.gpsimd.dma_start(w4_planes[32 * quad : 32 * quad + 4, :, :].bitcast(I32), w4_rows[4 * quad : 4 * quad + 4])
+
+        tab_sb = [keep.tile([P, T], U32, name=f"tab_sb{a}", align_bytes=64) for a in range(2)]
+        w1_raw = {}
+
+        def load_w1(a, b):
+            w1_raw[a, b] = keep.tile([P, PACK, K_PASS], F32, name=f"w1_raw{a}{b}", tag=f"w1_raw{a}")
+            rows = w1[a * K_PASS : (a + 1) * K_PASS, b * K_PASS : (b + 1) * K_PASS]
+            nc.sync.dma_start(w1_raw[a, b][:], rows.rearrange("(p j) c -> p j c", j=PACK))
+
+        for a in range(2):
+            nc.sync.dma_start(tab_sb[a][:].bitcast(I32), tab_words[a].rearrange("p t i -> p (t i)").bitcast(I32))
+            load_w1(a, 0)
+
+        picked_bytes = keep.tile([P, S], U8, name="picked_bytes", align_bytes=64)
+        nc.vector.tensor_copy(picked_bytes[:], tab_bytes[:].indirect(offs_sb[:]))
+        v_planes = keep.tile([P, S], U8, name="v_planes", align_bytes=64)
+        nc.vector.tensor_copy(v_planes[:].bitcast(I32), picked_bytes[:].bitcast(I32))
+        for a in range(2):
+            for e in range(2):
+                row = PLANE_ROW * a + e
+                nc.scalar.dma_start(
+                    v_planes[row + 2 : P : 32, :].bitcast(I32), picked_bytes[row + 16 : P : 32, :].bitcast(I32)
+                )
+
+
+        v_words = [keep.tile([P, S], U32, name=f"v_words{a}", align_bytes=64) for a in range(2)]
+        w1_codes, w1_planes = {}, {}
+
+        def quantize_w1(a, b, u, on_vector):
+            grouped = keep.tile([P, 2, P, PACK], BF16, name=f"w1_grouped{a}{b}{u}", tag=f"grouped{a}{b}{u}", align_bytes=64)
+            src = w1_raw[a, b][:].rearrange("p j (m t) -> p m j t", t=PACK)[:, :, :, 2 * u : 2 * u + 2]
+            dst = grouped[:].rearrange("p e m j -> p m j e")
+            if on_vector:
+                nc.vector.tensor_copy(dst, src)
+            else:
+                nc.scalar.copy(dst, src)
+            codes = keep.tile([P, 2 * P], U32, name=f"w1_codes{a}{b}{u}", align_bytes=64)
+            planes = keep.tile([P, 2 * P], U8, name=f"w1_planes{a}{b}{u}", align_bytes=64)
+            nc.vector.quantize_mx(codes[:].bitcast(FP8X4), planes[:], grouped[:].rearrange("p e m j -> p (e m j)"))
+            w1_codes[a, b, u], w1_planes[a, b, u] = codes, planes
+
+        def first_pass(acc, a, b, t, half):
+            u, e = divmod(t, 2)
+            rows = slice(e * P, (e + 1) * P)
+            cols = slice(half * BANK, (half + 1) * BANK)
+            nc.tensor.matmul_mx(
+                acc[:],
+                lhsT=w1_codes[a, b, u][:, rows].bitcast(FP8X4),
+                lhsT_scale=w1_planes[a, b, u][:, rows],
+                rhs=v_words[a][:, cols].bitcast(FP8X4),
+                rhs_scale=v_planes[PLANE_ROW * a : P, cols],
+                start=(a == 0),
+                stop=(a == 1),
+            )
+
+        def features(accs, b, t):
+            bent = ring.tile([P, S], F32, name="bent")
+            h = keep.tile([P, S], F32, name=f"h{b}{t}")
+            for half in range(2):
+                cols = slice(half * BANK, (half + 1) * BANK)
+                nc.scalar.activation(bent[:, cols], accs[half][:], ACT.Tanh, bias=bias_sb[:, b, t : t + 1])
+                if (b, t) == (0, 0):
+                    nc.vector.tensor_scalar(h[:, cols], bent[:, cols], gain_sb[:, b, t : t + 1], None, ALU.mult)
+            if (b, t) != (0, 0):
+                nc.scalar.activation(h[:], bent[:], ACT.Copy, scale=gain_sb[:, b, t : t + 1])
+            return h
+
+        def gather(dst, h, i, m0, m1):
+            nc.vector.tensor_copy(dst, h[:].indirect(pos_sb[i][:, m0 // 16 : m1 // 16]))
+
+        def quantize_z(picked, m0, m1, name):
+            width = m1 - m0
+            z = keep.tile([P, width, PACK], BF16, name=f"z{name}", align_bytes=64)
+            sides = [g[:, :, m0:m1].rearrange("p t (c i) -> p c t i", i=4) for g in picked]
+            nc.vector.tensor_tensor(z[:].rearrange("p (c i) t -> p c t i", i=4), sides[0], sides[1], ALU.max)
+            codes = keep.tile([P, width], U32, name=f"z_codes{name}", align_bytes=64)
+            planes = keep.tile([P, width], U8, name=f"z_planes{name}", align_bytes=64)
+            nc.vector.quantize_mx(codes[:].bitcast(FP8X4), planes[:], z[:].rearrange("p m t -> p (m t)"))
+            return codes, planes
+
+        def second_passes(acc, b, codes, planes):
+            for nt in range(N // P):
+                nc.tensor.matmul_mx(
+                    acc[:, nt * CHUNK : (nt + 1) * CHUNK],
+                    lhsT=w4_sb[:, b, 2 * nt * P : 2 * (nt + 1) * P].bitcast(FP4X4),
+                    lhsT_scale=w4_planes[:, b, nt * P : (nt + 1) * P],
+                    rhs=codes.bitcast(FP8X4),
+                    rhs_scale=planes,
+                    start=(b == 0 and nt == 0),
+                    stop=(b == 1 and nt == N // P - 1),
+                )
+
+        nc.vector.tensor_copy(v_words[0][:], tab_sb[0][:].indirect(offs_sb[:]))
+        for u in range(2):
+            quantize_w1(0, 0, u, False)
+        nc.vector.tensor_copy(v_words[1][:], tab_sb[1][:].indirect(offs_sb[:]))
+        accs = {(t, half): psum.tile([P, BANK], F32, name="acc") for t in range(PACK) for half in range(2)}
+        for t in range(PACK):
+            for half in range(2):
+                first_pass(accs[t, half], 0, 0, t, half)
+        for u in range(2):
+            quantize_w1(1, 0, u, u == 0)
+        for t in range(PACK):
+            for half in range(2):
+                first_pass(accs[t, half], 1, 0, t, half)
+        picked = [keep.tile([P, PACK, PAIRS], F32, name=f"picked0{i}") for i in range(2)]
+        for t in range(PACK):
+            h = features([accs[t, 0], accs[t, 1]], 0, t)
+            for i in range(2):
+                gather(picked[i][:, t, :], h, i, 0, PAIRS)
+        for a in range(2):
+            load_w1(a, 1)
+        w4_sb = keep.tile([P, 2, 2 * N], U8, name="w4_sb", tag="grouped101", align_bytes=64)
+        nc.sync.dma_start(w4_sb[:].bitcast(I32), w4_words.rearrange("a p n -> p a n").bitcast(I32))
+        for u in range(2):
+            for a in range(2):
+                quantize_w1(a, 1, u, False)
+        z0_codes, z0_planes = quantize_z(picked, 0, PAIRS, "0")
+
+        picked = [keep.tile([P, PACK, PAIRS], F32, name=f"picked1{i}") for i in range(2)]
+        for t in range(PACK):
+            pair = [psum.tile([P, BANK], F32, name="acc") for half in range(2)]
+            for half in range(2):
+                for a in range(2):
+                    first_pass(pair[half], a, 1, t, half)
+            h = features(pair, 1, t)
+            if t < PACK - 1:
+                for i in range(2):
+                    gather(picked[i][:, t, :], h, i, 0, PAIRS)
+
+        scores = [psum.tile([P, BANK], F32, name="acc") for c in range(PAIRS // CHUNK)]
+        for c in range(PAIRS // CHUNK):
+            cols = slice(c * CHUNK, (c + 1) * CHUNK)
+            second_passes(scores[c], 0, z0_codes[:, cols], z0_planes[:, cols])
+        out_rows = out.rearrange("(nt p) m -> p nt m", p=P)
+        for c in range(PAIRS // CHUNK):
+            m0, m1 = c * CHUNK, (c + 1) * CHUNK
+            for i in range(2):
+                gather(picked[i][:, PACK - 1, m0:m1], h, i, m0, m1)
+            codes, planes = quantize_z(picked, m0, m1, f"1{c}")
+            second_passes(scores[c], 1, codes[:], planes[:])
+            result = keep.tile([P, N // P, CHUNK], F32, name=f"result{c}")
+            nc.scalar.copy(result[:].rearrange("p nt m -> p (nt m)"), scores[c][:])
+            nc.sync.dma_start(out_rows[:, :, m0:m1], result[:])

@@ -60,28 +60,28 @@ def tile_list_braille_proof_scores_kernel(
         for quad in range(4):
             nc.gpsimd.dma_start(w4_planes[32 * quad : 32 * quad + 4, :, :].bitcast(I32), w4_rows[4 * quad : 4 * quad + 4])
 
-        tab_sb = [keep.tile([P, T], U32, name=f"tab_sb{a}", align_bytes=64) for a in range(2)]
+        tab_sb = [keep.tile([P, T], U32, name=f"tab_sb{a}", tag=f"tab_sb{a}", align_bytes=64) for a in range(2)]
         w1_raw = {}
 
-        def load_w1(a, b):
-            w1_raw[a, b] = keep.tile([P, PACK, K_PASS], F32, name=f"w1_raw{a}{b}", tag=f"w1_raw{a}")
+        def load_w1(a, b, tag):
+            w1_raw[a, b] = keep.tile([P, PACK, K_PASS], F32, name=f"w1_raw{a}{b}", tag=tag, align_bytes=64)
             rows = w1[a * K_PASS : (a + 1) * K_PASS, b * K_PASS : (b + 1) * K_PASS]
             nc.sync.dma_start(w1_raw[a, b][:], rows.rearrange("(p j) c -> p j c", j=PACK))
 
         for a in range(2):
             nc.sync.dma_start(tab_sb[a][:].bitcast(I32), tab_words[a].rearrange("p t i -> p (t i)").bitcast(I32))
-            load_w1(a, 0)
+            if a == 0:
+                load_w1(0, 0, "w1_raw00")
 
-        picked_bytes = keep.tile([P, S], U8, name="picked_bytes", align_bytes=64)
+        picked_bytes = keep.tile([P, S], U8, name="picked_bytes", tag="picked_bytes", align_bytes=64)
         nc.vector.tensor_copy(picked_bytes[:], tab_bytes[:].indirect(offs_sb[:]))
         v_planes = keep.tile([P, S], U8, name="v_planes", align_bytes=64)
         nc.vector.tensor_copy(v_planes[:].bitcast(I32), picked_bytes[:].bitcast(I32))
         for a in range(2):
             for e in range(2):
                 row = PLANE_ROW * a + e
-                nc.scalar.dma_start(
-                    v_planes[row + 2 : P : 32, :].bitcast(I32), picked_bytes[row + 16 : P : 32, :].bitcast(I32)
-                )
+                nc.sync.dma_start(v_planes[row + 2 : P : 32, :].bitcast(I32), v_planes[row + 16 : P : 32, :].bitcast(I32))
+        load_w1(1, 0, "picked_bytes")
 
 
         v_words = [keep.tile([P, S], U32, name=f"v_words{a}", align_bytes=64) for a in range(2)]
@@ -129,9 +129,9 @@ def tile_list_braille_proof_scores_kernel(
         def gather(dst, h, i, m0, m1):
             nc.vector.tensor_copy(dst, h[:].indirect(pos_sb[i][:, m0 // 16 : m1 // 16]))
 
-        def quantize_z(picked, m0, m1, name):
+        def quantize_z(picked, m0, m1, name, tag):
             width = m1 - m0
-            z = keep.tile([P, width, PACK], BF16, name=f"z{name}", align_bytes=64)
+            z = keep.tile([P, width, PACK], BF16, name=f"z{name}", tag=tag, align_bytes=64)
             sides = [g[:, :, m0:m1].rearrange("p t (c i) -> p c t i", i=4) for g in picked]
             nc.vector.tensor_tensor(z[:].rearrange("p (c i) t -> p c t i", i=4), sides[0], sides[1], ALU.max)
             codes = keep.tile([P, width], U32, name=f"z_codes{name}", align_bytes=64)
@@ -155,36 +155,33 @@ def tile_list_braille_proof_scores_kernel(
         for u in range(2):
             quantize_w1(0, 0, u, False)
         nc.vector.tensor_copy(v_words[1][:], tab_sb[1][:].indirect(offs_sb[:]))
-        accs = {(t, half): psum.tile([P, BANK], F32, name="acc") for t in range(PACK) for half in range(2)}
-        for t in range(PACK):
-            for half in range(2):
-                first_pass(accs[t, half], 0, 0, t, half)
         for u in range(2):
             quantize_w1(1, 0, u, u == 0)
-        for t in range(PACK):
-            for half in range(2):
-                first_pass(accs[t, half], 1, 0, t, half)
+
+        def first_product(b, t):
+            accs = [psum.tile([P, BANK], F32, name="acc") for half in range(2)]
+            for a in range(2):
+                for half in range(2):
+                    first_pass(accs[half], a, b, t, half)
+            return accs
+
         picked = [keep.tile([P, PACK, PAIRS], F32, name=f"picked0{i}") for i in range(2)]
         for t in range(PACK):
-            h = features([accs[t, 0], accs[t, 1]], 0, t)
+            h = features(first_product(0, t), 0, t)
             for i in range(2):
                 gather(picked[i][:, t, :], h, i, 0, PAIRS)
-        for a in range(2):
-            load_w1(a, 1)
+        load_w1(0, 1, "tab_sb0")
+        load_w1(1, 1, "w1_raw00")
         w4_sb = keep.tile([P, 2, 2 * N], U8, name="w4_sb", tag="grouped101", align_bytes=64)
         nc.sync.dma_start(w4_sb[:].bitcast(I32), w4_words.rearrange("a p n -> p a n").bitcast(I32))
         for u in range(2):
             for a in range(2):
-                quantize_w1(a, 1, u, False)
-        z0_codes, z0_planes = quantize_z(picked, 0, PAIRS, "0")
+                quantize_w1(a, 1, u, (a, u) == (0, 0))
+        z0_codes, z0_planes = quantize_z(picked, 0, PAIRS, "0", "grouped110")
 
         picked = [keep.tile([P, PACK, PAIRS], F32, name=f"picked1{i}") for i in range(2)]
         for t in range(PACK):
-            pair = [psum.tile([P, BANK], F32, name="acc") for half in range(2)]
-            for half in range(2):
-                for a in range(2):
-                    first_pass(pair[half], a, 1, t, half)
-            h = features(pair, 1, t)
+            h = features(first_product(1, t), 1, t)
             if t < PACK - 1:
                 for i in range(2):
                     gather(picked[i][:, t, :], h, i, 0, PAIRS)
@@ -198,7 +195,7 @@ def tile_list_braille_proof_scores_kernel(
             m0, m1 = c * CHUNK, (c + 1) * CHUNK
             for i in range(2):
                 gather(picked[i][:, PACK - 1, m0:m1], h, i, m0, m1)
-            codes, planes = quantize_z(picked, m0, m1, f"1{c}")
+            codes, planes = quantize_z(picked, m0, m1, f"1{c}", f"z1{c}")
             second_passes(scores[c], 1, codes[:], planes[:])
             result = keep.tile([P, N // P, CHUNK], F32, name=f"result{c}")
             nc.scalar.copy(result[:].rearrange("p nt m -> p (nt m)"), scores[c][:])

@@ -132,23 +132,25 @@ def tile_list_braille_proof_scores_kernel(
         def quantize_z(picked, m0, m1, name, tag):
             width = m1 - m0
             z = keep.tile([P, width, PACK], BF16, name=f"z{name}", tag=tag, align_bytes=64)
-            sides = [g[:, :, m0:m1].rearrange("p t (c i) -> p c t i", i=4) for g in picked]
-            nc.vector.tensor_tensor(z[:].rearrange("p (c i) t -> p c t i", i=4), sides[0], sides[1], ALU.max)
+            sides = [g[:, :, m0:m1].rearrange("p t (c i) -> p c t i", i=2) for g in picked]
+            nc.vector.tensor_tensor(z[:].rearrange("p (c i) t -> p c t i", i=2), sides[0], sides[1], ALU.max)
             codes = keep.tile([P, width], U32, name=f"z_codes{name}", align_bytes=64)
             planes = keep.tile([P, width], U8, name=f"z_planes{name}", align_bytes=64)
             nc.vector.quantize_mx(codes[:].bitcast(FP8X4), planes[:], z[:].rearrange("p m t -> p (m t)"))
             return codes, planes
 
-        def second_passes(acc, b, codes, planes):
+        def second_passes(banks, b, codes, planes):
+            share = N // P // len(banks)
             for nt in range(N // P):
+                place = nt % share
                 nc.tensor.matmul_mx(
-                    acc[:, nt * CHUNK : (nt + 1) * CHUNK],
+                    banks[nt // share][:, place * CHUNK : (place + 1) * CHUNK],
                     lhsT=w4_sb[:, b, 2 * nt * P : 2 * (nt + 1) * P].bitcast(FP4X4),
                     lhsT_scale=w4_planes[:, b, nt * P : (nt + 1) * P],
                     rhs=codes.bitcast(FP8X4),
                     rhs_scale=planes,
-                    start=(b == 0 and nt == 0),
-                    stop=(b == 1 and nt == N // P - 1),
+                    start=(b == 0 and place == 0),
+                    stop=(b == 1 and place == share - 1),
                 )
 
         nc.vector.tensor_copy(v_words[0][:], tab_sb[0][:].indirect(offs_sb[:]))
@@ -186,17 +188,26 @@ def tile_list_braille_proof_scores_kernel(
                 for i in range(2):
                     gather(picked[i][:, t, :], h, i, 0, PAIRS)
 
-        scores = [psum.tile([P, BANK], F32, name="acc") for c in range(PAIRS // CHUNK)]
-        for c in range(PAIRS // CHUNK):
+        chunks = PAIRS // CHUNK
+        scores = [
+            [psum.tile([P, BANK], F32, name="acc") for part in range(2 if c == chunks - 1 else 1)] for c in range(chunks)
+        ]
+        for c in range(chunks):
             cols = slice(c * CHUNK, (c + 1) * CHUNK)
             second_passes(scores[c], 0, z0_codes[:, cols], z0_planes[:, cols])
         out_rows = out.rearrange("(nt p) m -> p nt m", p=P)
-        for c in range(PAIRS // CHUNK):
+        for c in range(chunks):
             m0, m1 = c * CHUNK, (c + 1) * CHUNK
             for i in range(2):
                 gather(picked[i][:, PACK - 1, m0:m1], h, i, m0, m1)
             codes, planes = quantize_z(picked, m0, m1, f"1{c}", f"z1{c}")
             second_passes(scores[c], 1, codes[:], planes[:])
-            result = keep.tile([P, N // P, CHUNK], F32, name=f"result{c}")
-            nc.scalar.copy(result[:].rearrange("p nt m -> p (nt m)"), scores[c][:])
-            nc.sync.dma_start(out_rows[:, :, m0:m1], result[:])
+            share = N // P // len(scores[c])
+            for part, bank in enumerate(scores[c]):
+                result = keep.tile([P, share, CHUNK], F32, name=f"result{c}{part}")
+                flat = result[:].rearrange("p nt m -> p (nt m)")
+                if part == 0:
+                    nc.scalar.copy(flat, bank[:, : share * CHUNK])
+                else:
+                    nc.vector.tensor_copy(flat, bank[:, : share * CHUNK])
+                nc.sync.dma_start(out_rows[:, part * share : (part + 1) * share, m0:m1], result[:])

@@ -41,8 +41,6 @@ def tile_list_braille_proof_scores_kernel(
         nc.gpsimd.memset(tab_bytes[:].bitcast(I32), 0)
         warm = keep.tile([P, 2], F32, name="warm")
         nc.vector.memset(warm[:, 0:1], 0.0)
-        w4_planes = keep.tile([P, 2, N], U8, name="w4_planes", align_bytes=64)
-        nc.vector.memset(w4_planes[:].bitcast(I32), 0)
 
         nc.sync.dma_start(offs_sb[:], offs)
         nc.sync.dma_start(pos_sb[0][:], pos1)
@@ -56,9 +54,6 @@ def tile_list_braille_proof_scores_kernel(
         gain_sb = keep.tile([P, 2, PACK], F32, name="gain_sb")
         nc.gpsimd.dma_start(bias_sb[:], b1.rearrange("(b p t) -> p b t", b=2, t=PACK))
         nc.gpsimd.dma_start(gain_sb[:], gain.rearrange("(b p t) -> p b t", b=2, t=PACK))
-        w4_rows = w4_scales.rearrange("a q n -> q a n").bitcast(I32)
-        for quad in range(4):
-            nc.gpsimd.dma_start(w4_planes[32 * quad : 32 * quad + 4, :, :].bitcast(I32), w4_rows[4 * quad : 4 * quad + 4])
 
         tab_sb = [keep.tile([P, T], U32, name=f"tab_sb{a}", tag=f"tab_sb{a}", align_bytes=64) for a in range(2)]
         w1_raw = {}
@@ -87,27 +82,29 @@ def tile_list_braille_proof_scores_kernel(
         v_words = [keep.tile([P, S], U32, name=f"v_words{a}", align_bytes=64) for a in range(2)]
         w1_codes, w1_planes = {}, {}
 
-        def quantize_w1(a, b, u, on_vector):
-            grouped = keep.tile([P, 2, P, PACK], BF16, name=f"w1_grouped{a}{b}{u}", tag=f"grouped{a}{b}{u}", align_bytes=64)
-            src = w1_raw[a, b][:].rearrange("p j (m t) -> p m j t", t=PACK)[:, :, :, 2 * u : 2 * u + 2]
+        def quantize_w1(a, b, t0, t1, on_vector, codes_tag=None):
+            name = f"{a}{b}{t0}"
+            count = t1 - t0
+            grouped = keep.tile([P, count, P, PACK], BF16, name=f"w1_grouped{name}", tag=f"grouped{name}", align_bytes=64)
+            src = w1_raw[a, b][:].rearrange("p j (m t) -> p m j t", t=PACK)[:, :, :, t0:t1]
             dst = grouped[:].rearrange("p e m j -> p m j e")
             if on_vector:
                 nc.vector.tensor_copy(dst, src)
             else:
                 nc.scalar.copy(dst, src)
-            codes = keep.tile([P, 2 * P], U32, name=f"w1_codes{a}{b}{u}", align_bytes=64)
-            planes = keep.tile([P, 2 * P], U8, name=f"w1_planes{a}{b}{u}", align_bytes=64)
+            codes = keep.tile([P, count * P], U32, name=f"w1_codes{name}", tag=codes_tag or f"codes{name}", align_bytes=64)
+            planes = keep.tile([P, count * P], U8, name=f"w1_planes{name}", align_bytes=64)
             nc.vector.quantize_mx(codes[:].bitcast(FP8X4), planes[:], grouped[:].rearrange("p e m j -> p (e m j)"))
-            w1_codes[a, b, u], w1_planes[a, b, u] = codes, planes
+            for t in range(t0, t1):
+                rows = slice((t - t0) * P, (t - t0 + 1) * P)
+                w1_codes[a, b, t], w1_planes[a, b, t] = codes[:, rows], planes[:, rows]
 
         def first_pass(acc, a, b, t, half):
-            u, e = divmod(t, 2)
-            rows = slice(e * P, (e + 1) * P)
             cols = slice(half * BANK, (half + 1) * BANK)
             nc.tensor.matmul_mx(
                 acc[:],
-                lhsT=w1_codes[a, b, u][:, rows].bitcast(FP8X4),
-                lhsT_scale=w1_planes[a, b, u][:, rows],
+                lhsT=w1_codes[a, b, t].bitcast(FP8X4),
+                lhsT_scale=w1_planes[a, b, t],
                 rhs=v_words[a][:, cols].bitcast(FP8X4),
                 rhs_scale=v_planes[PLANE_ROW * a : P, cols],
                 start=(a == 0),
@@ -154,11 +151,12 @@ def tile_list_braille_proof_scores_kernel(
                 )
 
         nc.vector.tensor_copy(v_words[0][:], tab_sb[0][:].indirect(offs_sb[:]))
-        for u in range(2):
-            quantize_w1(0, 0, u, False)
+        quantize_w1(0, 0, 0, 2, False)
         nc.vector.tensor_copy(v_words[1][:], tab_sb[1][:].indirect(offs_sb[:]))
-        for u in range(2):
-            quantize_w1(1, 0, u, u == 0)
+        quantize_w1(1, 0, 0, 1, True)
+        quantize_w1(1, 0, 1, 2, True)
+        quantize_w1(0, 0, 2, 4, False, "grouped100")
+        quantize_w1(1, 0, 2, 4, False)
 
         def first_product(b, t):
             accs = [psum.tile([P, BANK], F32, name="acc") for half in range(2)]
@@ -173,12 +171,17 @@ def tile_list_braille_proof_scores_kernel(
             for i in range(2):
                 gather(picked[i][:, t, :], h, i, 0, PAIRS)
         load_w1(0, 1, "tab_sb0")
+        w4_planes = keep.tile([P, 2, N], U8, name="w4_planes", tag="grouped000", align_bytes=64)
+        nc.vector.memset(w4_planes[:].bitcast(I32), 0)
+        w4_rows = w4_scales.rearrange("a q n -> q a n").bitcast(I32)
+        for quad in range(4):
+            nc.sync.dma_start(w4_planes[32 * quad : 32 * quad + 4, :, :].bitcast(I32), w4_rows[4 * quad : 4 * quad + 4])
         load_w1(1, 1, "w1_raw00")
-        w4_sb = keep.tile([P, 2, 2 * N], U8, name="w4_sb", tag="grouped101", align_bytes=64)
+        w4_sb = keep.tile([P, 2, 2 * N], U8, name="w4_sb", tag="grouped102", align_bytes=64)
         nc.sync.dma_start(w4_sb[:].bitcast(I32), w4_words.rearrange("a p n -> p a n").bitcast(I32))
         for u in range(2):
             for a in range(2):
-                quantize_w1(a, 1, u, (a, u) == (0, 0))
+                quantize_w1(a, 1, 2 * u, 2 * u + 2, (a, u) == (0, 0))
         z0_codes, z0_planes = quantize_z(picked, 0, PAIRS, "0", "grouped110")
 
         picked = [keep.tile([P, PACK, PAIRS], F32, name=f"picked1{i}") for i in range(2)]

from contextlib import ExitStack

import concourse.mybir as mybir

K, T, S, PAIRS, H, N = 1024, 2048, 1024, 512, 1024, 512
FLOPS = 2 * K * H * S + 2 * H * N * PAIRS

F32 = mybir.dt.float32
BF16 = mybir.dt.bfloat16
I32 = mybir.dt.int32
U32 = mybir.dt.uint32
U16 = mybir.dt.uint16
U8 = mybir.dt.uint8
FP8X4 = mybir.dt.float8_e4m3fn_x4
FP4X4 = mybir.dt.float4_e2m1fn_x4
ACT = mybir.ActivationFunctionType
ALU = mybir.AluOpType

P = 128
PACK = 4
K_PASS = P * PACK
BANK = 512
CHUNK = 128
PLANE_ROW = 8


def tile_list_braille_proof_scores_kernel(
    tc, tab_words, tab_scales, offs, pos1, pos2, w1, b1, gain, w4_words, w4_scales, out
):
    nc = tc.nc
    with ExitStack() as ctx:
        lists = ctx.enter_context(tc.tile_pool(name="lists", bufs=1))
        keep = ctx.enter_context(tc.tile_pool(name="keep", bufs=1))
        ring = ctx.enter_context(tc.tile_pool(name="ring", bufs=2))
        psum = ctx.enter_context(tc.psum_pool(name="psum", bufs=8))

        offs_sb = lists.tile([P, S // 16], U16, name="offs_sb")
        pos_sb = [lists.tile([P, PAIRS // 16], U16, name=f"pos{i}_sb") for i in (1, 2)]

        tab_bytes = keep.tile([P, T], U8, name="tab_bytes", align_bytes=64)
        nc.gpsimd.memset(tab_bytes[:].bitcast(I32), 0)
        warm = keep.tile([P, 2], F32, name="warm")
        nc.vector.memset(warm[:, 0:1], 0.0)

        nc.sync.dma_start(offs_sb[:], offs)
        nc.sync.dma_start(pos_sb[0][:], pos1)
        nc.sync.dma_start(pos_sb[1][:], pos2)
        scale_rows = tab_scales.rearrange("a (g e) t -> e g a t", e=2).bitcast(I32)
        for e in range(2):
            nc.sync.dma_start(tab_bytes[e:P:PLANE_ROW, :].bitcast(I32), scale_rows[e])
        nc.scalar.activation(warm[:, 1:2], warm[:, 0:1], ACT.Tanh)

        bias_sb = keep.tile([P, 2, PACK], F32, name="bias_sb")
        gain_sb = keep.tile([P, 2, PACK], F32, name="gain_sb")
        nc.gpsimd.dma_start(bias_sb[:], b1.rearrange("(b p t) -> p b t", b=2, t=PACK))
        nc.gpsimd.dma_start(gain_sb[:], gain.rearrange("(b p t) -> p b t", b=2, t=PACK))

        tab_sb = [keep.tile([P, T], U32, name=f"tab_sb{a}", tag=f"tab_sb{a}", align_bytes=64) for a in range(2)]
        w1_raw = {}

        def load_w1(a, b, tag):
            w1_raw[a, b] = keep.tile([P, PACK, K_PASS], F32, name=f"w1_raw{a}{b}", tag=tag, align_bytes=64)
            rows = w1[a * K_PASS : (a + 1) * K_PASS, b * K_PASS : (b + 1) * K_PASS]
            nc.sync.dma_start(w1_raw[a, b][:], rows.rearrange("(p j) c -> p j c", j=PACK))

        for a in range(2):
            nc.sync.dma_start(tab_sb[a][:].bitcast(I32), tab_words[a].rearrange("p t i -> p (t i)").bitcast(I32))
            if a == 0:
                load_w1(0, 0, "w1_raw00")

        picked_bytes = keep.tile([P, S], U8, name="picked_bytes", tag="picked_bytes", align_bytes=64)
        nc.vector.tensor_copy(picked_bytes[:], tab_bytes[:].indirect(offs_sb[:]))
        v_planes = keep.tile([P, S], U8, name="v_planes", align_bytes=64)
        nc.vector.tensor_copy(v_planes[:].bitcast(I32), picked_bytes[:].bitcast(I32))
        for a in range(2):
            for e in range(2):
                row = PLANE_ROW * a + e
                nc.sync.dma_start(v_planes[row + 2 : P : 32, :].bitcast(I32), v_planes[row + 16 : P : 32, :].bitcast(I32))
        load_w1(1, 0, "picked_bytes")


        v_words = [keep.tile([P, S], U32, name=f"v_words{a}", align_bytes=64) for a in range(2)]
        w1_codes, w1_planes = {}, {}

        def quantize_w1(a, b, t0, t1, on_vector, codes_tag=None):
            name = f"{a}{b}{t0}"
            count = t1 - t0
            grouped = keep.tile([P, count, P, PACK], BF16, name=f"w1_grouped{name}", tag=f"grouped{name}", align_bytes=64)
            src = w1_raw[a, b][:].rearrange("p j (m t) -> p m j t", t=PACK)[:, :, :, t0:t1]
            dst = grouped[:].rearrange("p e m j -> p m j e")
            if on_vector:
                nc.vector.tensor_copy(dst, src)
            else:
                nc.scalar.copy(dst, src)
            codes = keep.tile([P, count * P], U32, name=f"w1_codes{name}", tag=codes_tag or f"codes{name}", align_bytes=64)
            planes = keep.tile([P, count * P], U8, name=f"w1_planes{name}", align_bytes=64)
            nc.vector.quantize_mx(codes[:].bitcast(FP8X4), planes[:], grouped[:].rearrange("p e m j -> p (e m j)"))
            for t in range(t0, t1):
                rows = slice((t - t0) * P, (t - t0 + 1) * P)
                w1_codes[a, b, t], w1_planes[a, b, t] = codes[:, rows], planes[:, rows]

        def first_pass(acc, a, b, t, half):
            cols = slice(half * BANK, (half + 1) * BANK)
            nc.tensor.matmul_mx(
                acc[:],
                lhsT=w1_codes[a, b, t].bitcast(FP8X4),
                lhsT_scale=w1_planes[a, b, t],
                rhs=v_words[a][:, cols].bitcast(FP8X4),
                rhs_scale=v_planes[PLANE_ROW * a : P, cols],
                start=(a == 0),
                stop=(a == 1),
            )

        def features(accs, b, t):
            bent = ring.tile([P, S], F32, name="bent")
            h = keep.tile([P, S], F32, name=f"h{b}{t}")
            for half in range(2):
                cols = slice(half * BANK, (half + 1) * BANK)
                nc.scalar.activation(bent[:, cols], accs[half][:], ACT.Tanh, bias=bias_sb[:, b, t : t + 1])
                if (b, t) == (0, 0):
                    nc.vector.tensor_scalar(h[:, cols], bent[:, cols], gain_sb[:, b, t : t + 1], None, ALU.mult)
            if (b, t) != (0, 0):
                nc.scalar.activation(h[:], bent[:], ACT.Copy, scale=gain_sb[:, b, t : t + 1])
            return h

        def gather(dst, h, i, m0, m1):
            nc.vector.tensor_copy(dst, h[:].indirect(pos_sb[i][:, m0 // 16 : m1 // 16]))

        def quantize_z(picked, m0, m1, name, tag):
            width = m1 - m0
            z = keep.tile([P, width, PACK], BF16, name=f"z{name}", tag=tag, align_bytes=64)
            sides = [g[:, :, m0:m1].rearrange("p t (c i) -> p c t i", i=2) for g in picked]
            nc.vector.tensor_tensor(z[:].rearrange("p (c i) t -> p c t i", i=2), sides[0], sides[1], ALU.max)
            codes = keep.tile([P, width], U32, name=f"z_codes{name}", align_bytes=64)
            planes = keep.tile([P, width], U8, name=f"z_planes{name}", align_bytes=64)
            nc.vector.quantize_mx(codes[:].bitcast(FP8X4), planes[:], z[:].rearrange("p m t -> p (m t)"))
            return codes, planes

        def second_passes(banks, b, codes, planes):
            share = N // P // len(banks)
            for nt in range(N // P):
                place = nt % share
                nc.tensor.matmul_mx(
                    banks[nt // share][:, place * CHUNK : (place + 1) * CHUNK],
                    lhsT=w4_sb[:, b, 2 * nt * P : 2 * (nt + 1) * P].bitcast(FP4X4),
                    lhsT_scale=w4_planes[:, b, nt * P : (nt + 1) * P],
                    rhs=codes.bitcast(FP8X4),
                    rhs_scale=planes,
                    start=(b == 0 and place == 0),
                    stop=(b == 1 and place == share - 1),
                )

        nc.vector.tensor_copy(v_words[0][:], tab_sb[0][:].indirect(offs_sb[:]))
        quantize_w1(0, 0, 0, 2, False)
        nc.vector.tensor_copy(v_words[1][:], tab_sb[1][:].indirect(offs_sb[:]))
        quantize_w1(1, 0, 0, 1, True)
        quantize_w1(1, 0, 1, 2, True)
        quantize_w1(0, 0, 2, 4, False, "grouped100")
        quantize_w1(1, 0, 2, 4, False)

        def first_product(b, t):
            accs = [psum.tile([P, BANK], F32, name="acc") for half in range(2)]
            for a in range(2):
                for half in range(2):
                    first_pass(accs[half], a, b, t, half)
            return accs

        picked = [keep.tile([P, PACK, PAIRS], F32, name=f"picked0{i}") for i in range(2)]
        for t in range(PACK):
            h = features(first_product(0, t), 0, t)
            for i in range(2):
                gather(picked[i][:, t, :], h, i, 0, PAIRS)
        load_w1(0, 1, "tab_sb0")
        w4_planes = keep.tile([P, 2, N], U8, name="w4_planes", tag="grouped000", align_bytes=64)
        nc.vector.memset(w4_planes[:].bitcast(I32), 0)
        w4_rows = w4_scales.rearrange("a q n -> q a n").bitcast(I32)
        for quad in range(4):
            nc.sync.dma_start(w4_planes[32 * quad : 32 * quad + 4, :, :].bitcast(I32), w4_rows[4 * quad : 4 * quad + 4])
        load_w1(1, 1, "w1_raw00")
        w4_sb = keep.tile([P, 2, 2 * N], U8, name="w4_sb", tag="grouped102", align_bytes=64)
        nc.sync.dma_start(w4_sb[:].bitcast(I32), w4_words.rearrange("a p n -> p a n").bitcast(I32))
        for u in range(2):
            for a in range(2):
                quantize_w1(a, 1, 2 * u, 2 * u + 2, (a, u) == (0, 0))
        z0_codes, z0_planes = quantize_z(picked, 0, PAIRS, "0", "grouped110")

        picked = [keep.tile([P, PACK, PAIRS], F32, name=f"picked1{i}") for i in range(2)]
        for t in range(PACK):
            h = features(first_product(1, t), 1, t)
            if t < PACK - 1:
                for i in range(2):
                    gather(picked[i][:, t, :], h, i, 0, PAIRS)

        chunks = PAIRS // CHUNK
        scores = [
            [psum.tile([P, BANK], F32, name="acc") for part in range(2 if c == chunks - 1 else 1)] for c in range(chunks)
        ]
        for c in range(chunks):
            cols = slice(c * CHUNK, (c + 1) * CHUNK)
            second_passes(scores[c], 0, z0_codes[:, cols], z0_planes[:, cols])
        out_rows = out.rearrange("(nt p) m -> p nt m", p=P)
        for c in range(chunks):
            m0, m1 = c * CHUNK, (c + 1) * CHUNK
            for i in range(2):
                gather(picked[i][:, PACK - 1, m0:m1], h, i, m0, m1)
            codes, planes = quantize_z(picked, m0, m1, f"1{c}", f"z1{c}")
            second_passes(scores[c], 1, codes[:], planes[:])
            share = N // P // len(scores[c])
            for part, bank in enumerate(scores[c]):
                result = keep.tile([P, share, CHUNK], F32, name=f"result{c}{part}")
                flat = result[:].rearrange("p nt m -> p (nt m)")
                if part == 0:
                    nc.scalar.copy(flat, bank[:, : share * CHUNK])
                else:
                    nc.vector.tensor_copy(flat, bank[:, : share * CHUNK])
                nc.sync.dma_start(out_rows[:, part * share : (part + 1) * share, m0:m1], result[:])
